import numpy as np
import ml_dtypes


def mxq(x, axis, fmt="e4m3"):
    dtype, down = {"e4m3": (ml_dtypes.float8_e4m3fn, 7), "e5m2": (ml_dtypes.float8_e5m2, 14)}[fmt]
    v = np.moveaxis(np.asarray(x, np.float32).astype(ml_dtypes.bfloat16).astype(np.float64), axis, -1)
    blocks = v.reshape(v.shape[:-1] + (-1, 32))
    amax = np.abs(blocks).max(-1, keepdims=True)
    byte = np.maximum(np.where(amax > 0, np.frexp(amax)[1] - 1 + 127, 0) - down, 1)
    scale = np.exp2(byte - 127.0)
    codes = (blocks / scale).astype(np.float32).astype(dtype).astype(np.float64)
    return np.moveaxis((codes * scale).reshape(v.shape), -1, axis)


WIDE = False


def mx_kscale(k):
    if not WIDE:
        return np.ones(k)
    levels = np.array([10, -10, 5, -5, 0])
    if k % 512:
        return np.exp2(np.random.permutation(np.resize(levels, k // 32))).repeat(32)
    a = np.empty((k // 512, 16))
    for p in range(k // 512):
        a[p, :8] = np.random.permutation(np.resize(levels, 8))
        for g in range(8):
            far = levels[np.abs(levels - a[p, g]) >= 10]
            a[p, g + 8] = far[np.random.randint(len(far))]
    return np.exp2(a.ravel()).repeat(32)


def f64(x):
    return np.asarray(x).astype(np.float64)


def striped(idx):
    return np.tile(np.asarray(idx).reshape(-1, 16).T, (8, 1)).astype(np.uint16)


def unstriped(offs):
    return offs[:16].T.reshape(-1).astype(np.int64)


E2M1 = np.array([0.0, 0.5, 1.0, 1.5, 2.0, 3.0, 4.0, 6.0, -0.0, -0.5, -1.0, -1.5, -2.0, -3.0, -4.0, -6.0])


def pack_weight(w, fmt):
    k, n = w.shape
    w = f64(np.asarray(w, np.float32).astype(ml_dtypes.bfloat16)).reshape(k // 32, 32, n)
    amax = np.abs(w).max(1)
    if fmt == "e4m3":
        byte = np.frexp(amax)[1] - 1 + 127 - 7
    else:
        mant, ex = np.frexp(amax / 6.0)
        byte = np.where(mant > 0.5, ex, ex - 1) + 127
    byte = np.clip(np.where(amax > 0, byte, 1), 1, 254)
    scaled = (w * np.exp2(127.0 - byte)[:, None, :]).reshape(k, n).astype(np.float32)
    by_word = np.ascontiguousarray(scaled.reshape(k // 512, 128, 4, n).transpose(0, 1, 3, 2))
    if fmt == "e4m3":
        words = by_word.astype(ml_dtypes.float8_e4m3fn).view(np.uint8)
    else:
        c = by_word.astype(ml_dtypes.float4_e2m1fn).view(np.uint8) & 0xF
        words = (c[..., 0::2] | (c[..., 1::2] << 4)).reshape(k // 512, 128, 2 * n)
    return np.ascontiguousarray(words), np.ascontiguousarray(byte.astype(np.uint8).reshape(k // 512, 16, n))


def unpack_weight(words, scales, fmt):
    g, _, n = scales.shape
    words = np.ascontiguousarray(words).reshape(g, 128, n, -1)
    if fmt == "e4m3":
        vals = words.view(ml_dtypes.float8_e4m3fn).astype(np.float64)
    else:
        nib = np.empty((g, 128, n, 4), np.uint8)
        nib[..., 0::2] = words & 0xF
        nib[..., 1::2] = words >> 4
        vals = E2M1[nib]
    vals = vals * np.repeat(np.exp2(scales.astype(np.float64) - 127.0), 8, axis=1)[..., None]
    return vals.transpose(0, 1, 3, 2).reshape(g * 512, n)


D, T, I, Q, J, U, M = 512, 2048, 512, 128, 512, 1024, 2048


def setup_inputs():
    n = np.random.standard_normal
    idx = np.random.permutation(T)[:I]
    idx2 = np.random.permutation(U)[:J]
    idx3 = np.random.permutation(M)[:I]
    fd = mx_kscale(D)
    fj = mx_kscale(J)
    tiesp = pack_weight(n((J, T)) * 0.08 / fj[:, None], "e4m3")
    return {
        "query": (n((D, Q)) * 1.0 / np.sqrt(D) * fd[:, None]).astype(np.float32),
        "hubs": (n((D, U)) / fd[:, None]).astype(np.float32),
        "hf": (np.random.uniform(0.5, 2.0, (J, 1)) * fj[:, None]).astype(np.float32),
        "ties_words": tiesp[0],
        "ties_scales": tiesp[1],
        "old": (np.random.uniform(0.0, 2.0, (Q, M))).astype(np.float32),
        "fade": (np.random.uniform(0.3, 0.9, (Q, 1))).astype(np.float32),
        "offs": striped(idx),
        "offs2": striped(idx2),
        "offs3": striped(idx3),
    }


def reference(query, hubs, hf, ties_words, ties_scales, old, fade, offs, offs2, offs3):
    idx = unstriped(offs)
    idx2 = unstriped(offs2)
    idx3 = unstriped(offs3)
    tiesu = unpack_weight(ties_words, ties_scales, "e4m3")
    hubsidx2q = mxq(f64(hubs)[:, idx2], 0, "e4m3")
    queryq = mxq(f64(query), 0, "e4m3")
    hb = hubsidx2q.T @ queryq
    hp = np.maximum(hb, 0.0) * f64(hf)
    hpq = mxq(hp, 0, "e4m3")
    tiesidxg = tiesu[:, idx]
    s = hpq.T @ tiesidxg
    p = np.exp(s - np.max(s, axis=1, keepdims=True))
    w = p / np.sum(p, axis=1, keepdims=True)
    ws = w * 256.0
    wf = np.zeros((Q, M))
    wf[:, idx3] = ws
    y = f64(old) * f64(fade) + wf
    return y

@@ -1,0 +1,143 @@
+from contextlib import ExitStack
+
+import concourse.mybir as mybir
+
+D, T, I, Q, J, U, M = 512, 2048, 512, 128, 512, 1024, 2048
+FLOPS = 2 * D * J * Q + 2 * J * Q * I
+
+F32 = mybir.dt.float32
+BF16 = mybir.dt.bfloat16
+I32 = mybir.dt.int32
+U32 = mybir.dt.uint32
+U16 = mybir.dt.uint16
+U8 = mybir.dt.uint8
+FP8X4 = mybir.dt.float8_e4m3fn_x4
+ALU = mybir.AluOpType
+ACT = mybir.ActivationFunctionType
+P = 128
+PACK = 4
+
+HUB_CHUNKS = [(0, 0, 512, "s"), (0, 512, 512, "v"),
+              (1, 0, 512, "s"), (1, 512, 256, "s"), (1, 768, 256, "v")]
+OUT_CHUNKS = [512, 512, 512, 256, 256]
+
+
+def tile_attend_relayed_soft_counts_kernel(tc, query, hubs, hf, ties_words, ties_scales, old, fade, offs, offs2, offs3, out):
+    nc = tc.nc
+    with ExitStack() as ctx:
+        sb = ctx.enter_context(tc.tile_pool(name="sb", bufs=1))
+        psum = ctx.enter_context(tc.psum_pool(name="psum", bufs=1))
+
+        tie_list = sb.tile([P, I // 16], U16, name="tie_list")
+        hub_list = sb.tile([P, J // 16], U16, name="hub_list")
+        place_list = sb.tile([P, I // 16], U16, name="place_list")
+
+        tie_bytes = sb.tile([P, T], U8, name="tie_bytes", align_bytes=64)
+        nc.vector.memset(tie_bytes[:].bitcast(I32), 0)
+        placed = sb.tile([P, M], F32, name="placed", align_bytes=64)
+        nc.vector.memset(placed[:], 0.0)
+
+        warm_in = sb.tile([P, 1], F32, name="warm_in")
+        warm_out = sb.tile([P, 1], F32, name="warm_out")
+        nc.gpsimd.memset(warm_in[:], 0.0)
+        nc.scalar.activation(out=warm_out[:], in_=warm_in[:], func=ACT.Exp)
+
+        nc.sync.dma_start(tie_list[:], offs)
+        for r in range(4):
+            nc.sync.dma_start(tie_bytes[r:P:32, :].bitcast(I32), ties_scales[0, r:16:4, :].bitcast(I32))
+
+        hub_rows = hubs.rearrange("(p t) u -> p t u", t=PACK)
+        raw = []
+        for n, (pair, c0, w, eng) in enumerate(HUB_CHUNKS):
+            t = sb.tile([P, 2, w], F32, name="hub_raw%d" % n, align_bytes=64)
+            nc.sync.dma_start(t[:], hub_rows[:, 2 * pair:2 * pair + 2, c0:c0 + w])
+            raw.append(t)
+            if n == 1:
+                nc.sync.dma_start(hub_list[:], offs2)
+
+        q_raw = sb.tile([P, PACK, Q], F32, name="q_raw", align_bytes=64)
+        nc.sync.dma_start(q_raw[:], query.rearrange("(p t) q -> p t q", t=PACK))
+        tie_words = sb.tile([P, T], I32, name="tie_words", align_bytes=64)
+        nc.sync.dma_start(tie_words[:], ties_words[0].rearrange("p n t -> p (n t)").bitcast(I32))
+        hf_sb = sb.tile([P, PACK], F32, name="hf_sb")
+        nc.sync.dma_start(hf_sb[:], hf.rearrange("(p r) o -> p (r o)", r=PACK))
+        nc.sync.dma_start(place_list[:], offs3)
+        fade_sb = sb.tile([P, 1], F32, name="fade_sb")
+        nc.sync.dma_start(fade_sb[:], fade)
+        old_sb = sb.tile([P, M], F32, name="old_sb", align_bytes=64)
+        nc.sync.dma_start(old_sb[:], old)
+
+        got_bytes = sb.tile([P, I], U8, name="got_bytes", align_bytes=64)
+        nc.vector.tensor_copy(out=got_bytes[:], in_=tie_bytes[:].indirect(tie_list[:]))
+
+        hub_bf = sb.tile([P, J * PACK], BF16, name="hub_bf", align_bytes=64)
+        dealt = hub_bf[:].bitcast(U32).rearrange("p (r m u) -> p u m r", r=PACK, u=2)
+        pairs = [sb.tile([P, U * 2], BF16, name="pair%d" % u, align_bytes=64) for u in range(2)]
+        for u in range(2):
+            for n, (pair, c0, w, eng) in enumerate(HUB_CHUNKS):
+                if pair != u:
+                    continue
+                dst = pairs[u][:, 2 * c0:2 * (c0 + w)].rearrange("p (c t) -> p c t", t=2)
+                src = raw[n][:].rearrange("p t c -> p c t")
+                if eng == "s":
+                    nc.scalar.activation(out=dst, in_=src, func=ACT.Copy)
+                else:
+                    nc.vector.tensor_copy(out=dst, in_=src)
+            nc.vector.tensor_copy(out=dealt[:, u], in_=pairs[u][:].bitcast(U32).indirect(hub_list[:]))
+
+        q_bf = sb.tile([P, Q, PACK], BF16, name="q_bf", align_bytes=64)
+        nc.scalar.activation(out=q_bf[:], in_=q_raw[:].rearrange("p t q -> p q t"), func=ACT.Copy)
+        q_codes = sb.tile([P, Q], U32, name="q_codes", align_bytes=64)
+        q_scales = sb.tile([P, Q], U8, name="q_scales", align_bytes=64)
+        nc.vector.quantize_mx(out=q_codes[:].bitcast(FP8X4), scales=q_scales[:], in_=q_bf[:].rearrange("p q t -> p (q t)"))
+
+        h_codes = sb.tile([P, J], U32, name="h_codes", align_bytes=64)
+        h_scales = sb.tile([P, J], U8, name="h_scales", align_bytes=64)
+        hb = psum.tile([P, PACK, Q], F32, name="hb")
+        for r in range(PACK):
+            cols = slice(r * P, (r + 1) * P)
+            nc.vector.quantize_mx(out=h_codes[:, cols].bitcast(FP8X4), scales=h_scales[:, cols],
+                                  in_=hub_bf[:, r * P * PACK:(r + 1) * P * PACK])
+            nc.tensor.matmul_mx(out=hb[:, r, :], lhsT=h_codes[:, cols].bitcast(FP8X4), lhsT_scale=h_scales[:, cols],
+                                rhs=q_codes[:].bitcast(FP8X4), rhs_scale=q_scales[:], start=True, stop=True)
+
+        H = I // 2
+        words_lo = sb.tile([P, H], U32, name="words_lo", align_bytes=64)
+        nc.vector.tensor_copy(out=words_lo[:], in_=tie_words[:].bitcast(U32).indirect(tie_list[:, 0:H // 16]))
+
+        hp_bf = sb.tile([P, Q, PACK], BF16, name="hp_bf", tag="hp_then_words", align_bytes=64)
+        nc.vector.scalar_tensor_tensor(out=hp_bf[:], in0=hb[:].rearrange("p r q -> p q r"), scalar=0.0,
+                                       in1=hf_sb[:].unsqueeze(1).to_broadcast([P, Q, PACK]), op0=ALU.max, op1=ALU.mult)
+        hp_codes = sb.tile([P, Q], U32, name="hp_codes", align_bytes=64)
+        hp_scales = sb.tile([P, Q], U8, name="hp_scales", align_bytes=64)
+        nc.vector.quantize_mx(out=hp_codes[:].bitcast(FP8X4), scales=hp_scales[:], in_=hp_bf[:].rearrange("p q t -> p (q t)"))
+        words_hi = sb.tile([P, H], U32, name="words_hi", tag="hp_then_words", align_bytes=64)
+        nc.vector.tensor_copy(out=words_hi[:], in_=tie_words[:].bitcast(U32).indirect(tie_list[:, H // 16:I // 16]))
+
+        s = psum.tile([P, I], F32, name="s")
+        for h, words in enumerate((words_lo, words_hi)):
+            cols = slice(h * H, (h + 1) * H)
+            nc.tensor.matmul_mx(out=s[:, cols], lhsT=hp_codes[:].bitcast(FP8X4), lhsT_scale=hp_scales[:],
+                                rhs=words[:].bitcast(FP8X4), rhs_scale=got_bytes[:, cols], start=True, stop=True)
+
+        neg_max = sb.tile([P, 1], F32, name="neg_max")
+        nc.vector.tensor_reduce(out=neg_max[:], in_=s[:], axis=mybir.AxisListType.X, op=ALU.max, negate=True)
+        p = sb.tile([P, I], F32, name="p", align_bytes=64)
+        total = sb.tile([P, 1], F32, name="total")
+        nc.scalar.activation(out=p[:], in_=s[:], func=ACT.Exp, bias=neg_max[:], accum_out=total[:])
+        inv = sb.tile([P, 1], F32, name="inv")
+        nc.vector.reciprocal(out=inv[:], in_=total[:])
+        nc.vector.tensor_copy(out=placed[:].indirect(place_list[:]), in_=p[:])
+        gain = sb.tile([P, 1], F32, name="gain")
+        nc.scalar.activation(out=gain[:], in_=inv[:], func=ACT.Copy, scale=256.0)
+
+        c0 = 0
+        for n, w in enumerate(OUT_CHUNKS):
+            cols = slice(c0, c0 + w)
+            faded = sb.tile([P, w], F32, name="faded%d" % n, align_bytes=64)
+            nc.scalar.activation(out=faded[:], in_=old_sb[:, cols], func=ACT.Copy, scale=fade_sb[:])
+            res = sb.tile([P, w], F32, name="res%d" % n, align_bytes=64)
+            nc.vector.scalar_tensor_tensor(out=res[:], in0=placed[:, cols], scalar=gain[:], in1=faded[:],
+                                           op0=ALU.mult, op1=ALU.add)
+            nc.sync.dma_start(out[:, cols], res[:])
+            c0 = c0 + w

@@ -17,9 +17,9 @@ ACT = mybir.ActivationFunctionType
 P = 128
 PACK = 4
 
-HUB_CHUNKS = [(0, 0, 512, "s"), (0, 512, 512, "v"),
-              (1, 0, 512, "s"), (1, 512, 256, "s"), (1, 768, 256, "v")]
-OUT_CHUNKS = [512, 512, 512, 256, 256]
+HUB_LOADS = [(0, 0, 512), (0, 512, 512), (1, 0, 512), (1, 512, 256), (1, 768, 256)]
+HUB_CASTS = [(0, 0, 512, "s"), (1, 0, 352, "v"), (1, 352, 160, "s"), (2, 0, 512, "s"), (3, 0, 256, "s"), (4, 0, 256, "v")]
+OUT_CHUNKS = [512, 512, 512, 384, 128]
 
 
 def tile_attend_relayed_soft_counts_kernel(tc, query, hubs, hf, ties_words, ties_scales, old, fade, offs, offs2, offs3, out):
@@ -34,6 +34,8 @@ def tile_attend_relayed_soft_counts_kernel(tc, query, hubs, hf, ties_words, ties
 
         tie_bytes = sb.tile([P, T], U8, name="tie_bytes", align_bytes=64)
         nc.vector.memset(tie_bytes[:].bitcast(I32), 0)
+        tie_plane = sb.tile([P, I], U8, name="tie_plane", align_bytes=64)
+        nc.vector.memset(tie_plane[:].bitcast(I32), 0)
         placed = sb.tile([P, M], F32, name="placed", align_bytes=64)
         nc.vector.memset(placed[:], 0.0)
 
@@ -42,23 +44,25 @@ def tile_attend_relayed_soft_counts_kernel(tc, query, hubs, hf, ties_words, ties
         nc.gpsimd.memset(warm_in[:], 0.0)
         nc.scalar.activation(out=warm_out[:], in_=warm_in[:], func=ACT.Exp)
 
-        nc.sync.dma_start(tie_list[:], offs)
-        for r in range(4):
-            nc.sync.dma_start(tie_bytes[r:P:32, :].bitcast(I32), ties_scales[0, r:16:4, :].bitcast(I32))
-
         hub_rows = hubs.rearrange("(p t) u -> p t u", t=PACK)
         raw = []
-        for n, (pair, c0, w, eng) in enumerate(HUB_CHUNKS):
+        for n, (pair, c0, w) in enumerate(HUB_LOADS):
             t = sb.tile([P, 2, w], F32, name="hub_raw%d" % n, align_bytes=64)
             nc.sync.dma_start(t[:], hub_rows[:, 2 * pair:2 * pair + 2, c0:c0 + w])
             raw.append(t)
-            if n == 1:
+            if n == 0:
+                nc.sync.dma_start(tie_list[:], offs)
+                nc.sync.dma_start(tie_bytes[0:P:8, :].bitcast(I32), ties_scales[0].bitcast(I32))
                 nc.sync.dma_start(hub_list[:], offs2)
 
         q_raw = sb.tile([P, PACK, Q], F32, name="q_raw", align_bytes=64)
         nc.sync.dma_start(q_raw[:], query.rearrange("(p t) q -> p t q", t=PACK))
         tie_words = sb.tile([P, T], I32, name="tie_words", align_bytes=64)
         nc.sync.dma_start(tie_words[:], ties_words[0].rearrange("p n t -> p (n t)").bitcast(I32))
+        got_bytes = sb.tile([P, I], U8, name="got_bytes", align_bytes=64)
+        nc.vector.tensor_copy(out=got_bytes[:], in_=tie_bytes[:].indirect(tie_list[:]))
+        for r in range(4):
+            nc.sync.dma_start(tie_plane[r:P:32, :].bitcast(I32), got_bytes[8 * r:P:32, :].bitcast(I32))
         hf_sb = sb.tile([P, PACK], F32, name="hf_sb")
         nc.sync.dma_start(hf_sb[:], hf.rearrange("(p r) o -> p (r o)", r=PACK))
         nc.sync.dma_start(place_list[:], offs3)
@@ -67,18 +71,18 @@ def tile_attend_relayed_soft_counts_kernel(tc, query, hubs, hf, ties_words, ties
         old_sb = sb.tile([P, M], F32, name="old_sb", align_bytes=64)
         nc.sync.dma_start(old_sb[:], old)
 
-        got_bytes = sb.tile([P, I], U8, name="got_bytes", align_bytes=64)
-        nc.vector.tensor_copy(out=got_bytes[:], in_=tie_bytes[:].indirect(tie_list[:]))
 
         hub_bf = sb.tile([P, J * PACK], BF16, name="hub_bf", align_bytes=64)
         dealt = hub_bf[:].bitcast(U32).rearrange("p (r m u) -> p u m r", r=PACK, u=2)
         pairs = [sb.tile([P, U * 2], BF16, name="pair%d" % u, align_bytes=64) for u in range(2)]
         for u in range(2):
-            for n, (pair, c0, w, eng) in enumerate(HUB_CHUNKS):
+            for n, a, w, eng in HUB_CASTS:
+                pair, base, whole = HUB_LOADS[n]
                 if pair != u:
                     continue
+                c0 = base + a
                 dst = pairs[u][:, 2 * c0:2 * (c0 + w)].rearrange("p (c t) -> p c t", t=2)
-                src = raw[n][:].rearrange("p t c -> p c t")
+                src = raw[n][:, :, a:a + w].rearrange("p t c -> p c t")
                 if eng == "s":
                     nc.scalar.activation(out=dst, in_=src, func=ACT.Copy)
                 else:
@@ -114,22 +118,25 @@ def tile_attend_relayed_soft_counts_kernel(tc, query, hubs, hf, ties_words, ties
         words_hi = sb.tile([P, H], U32, name="words_hi", tag="hp_then_words", align_bytes=64)
         nc.vector.tensor_copy(out=words_hi[:], in_=tie_words[:].bitcast(U32).indirect(tie_list[:, H // 16:I // 16]))
 
-        s = psum.tile([P, I], F32, name="s")
+        s = [psum.tile([P, H], F32, name="s%d" % h) for h in range(2)]
         for h, words in enumerate((words_lo, words_hi)):
-            cols = slice(h * H, (h + 1) * H)
-            nc.tensor.matmul_mx(out=s[:, cols], lhsT=hp_codes[:].bitcast(FP8X4), lhsT_scale=hp_scales[:],
-                                rhs=words[:].bitcast(FP8X4), rhs_scale=got_bytes[:, cols], start=True, stop=True)
+            nc.tensor.matmul_mx(out=s[h][:], lhsT=hp_codes[:].bitcast(FP8X4), lhsT_scale=hp_scales[:],
+                                rhs=words[:].bitcast(FP8X4), rhs_scale=tie_plane[:, h * H:(h + 1) * H], start=True, stop=True)
 
+        neg_lo = sb.tile([P, 1], F32, name="neg_lo")
+        nc.vector.tensor_reduce(out=neg_lo[:], in_=s[0][:], axis=mybir.AxisListType.X, op=ALU.max, negate=True)
         neg_max = sb.tile([P, 1], F32, name="neg_max")
-        nc.vector.tensor_reduce(out=neg_max[:], in_=s[:], axis=mybir.AxisListType.X, op=ALU.max, negate=True)
+        neg_hi = sb.tile([P, H], F32, name="neg_hi", align_bytes=64)
+        nc.vector.tensor_scalar(out=neg_hi[:], in0=s[1][:], scalar1=-1.0, scalar2=neg_lo[:], op0=ALU.mult, op1=ALU.min, accum_out=neg_max[:])
         p = sb.tile([P, I], F32, name="p", align_bytes=64)
+        for h in range(2):
+            nc.scalar.activation(out=p[:, h * H:(h + 1) * H], in_=s[h][:], func=ACT.Exp, bias=neg_max[:])
+        p_small = sb.tile([P, I], F32, name="p_small", align_bytes=64)
         total = sb.tile([P, 1], F32, name="total")
-        nc.scalar.activation(out=p[:], in_=s[:], func=ACT.Exp, bias=neg_max[:], accum_out=total[:])
-        inv = sb.tile([P, 1], F32, name="inv")
-        nc.vector.reciprocal(out=inv[:], in_=total[:])
+        nc.scalar.activation(out=p_small[:], in_=p[:], func=ACT.Copy, scale=1.0 / 256.0, accum_out=total[:])
         nc.vector.tensor_copy(out=placed[:].indirect(place_list[:]), in_=p[:])
         gain = sb.tile([P, 1], F32, name="gain")
-        nc.scalar.activation(out=gain[:], in_=inv[:], func=ACT.Copy, scale=256.0)
+        nc.vector.reciprocal(out=gain[:], in_=total[:])
 
         c0 = 0
         for n, w in enumerate(OUT_CHUNKS):

@@ -17,9 +17,8 @@ ACT = mybir.ActivationFunctionType
 P = 128
 PACK = 4
 
-HUB_LOADS = [(0, 0, 512), (0, 512, 512), (1, 0, 512), (1, 512, 256), (1, 768, 256)]
-HUB_CASTS = [(0, 0, 512, "s"), (1, 0, 352, "v"), (1, 352, 160, "s"), (2, 0, 512, "s"), (3, 0, 256, "s"), (4, 0, 256, "v")]
-OUT_CHUNKS = [512, 512, 512, 384, 128]
+PAIR_LOADS = [(0, 512), (512, 256), (768, 256)]
+OUT_CHUNKS = [256, 512, 512, 512, 256]
 
 
 def tile_attend_relayed_soft_counts_kernel(tc, query, hubs, hf, ties_words, ties_scales, old, fade, offs, offs2, offs3, out):
@@ -45,26 +44,33 @@ def tile_attend_relayed_soft_counts_kernel(tc, query, hubs, hf, ties_words, ties
         nc.scalar.activation(out=warm_out[:], in_=warm_in[:], func=ACT.Exp)
 
         hub_rows = hubs.rearrange("(p t) u -> p t u", t=PACK)
+        plane_raw = [sb.tile([P, U], F32, name="plane_raw%d" % t, align_bytes=64) for t in range(2)]
+        nc.sync.dma_start(plane_raw[0][:], hub_rows[:, 0, :])
+        nc.sync.dma_start(hub_list[:], offs2)
+        nc.sync.dma_start(tie_list[:], offs)
+        nc.sync.dma_start(tie_bytes[0:P:8, :].bitcast(I32), ties_scales[0].bitcast(I32))
+        nc.sync.dma_start(plane_raw[1][:], hub_rows[:, 1, :])
         raw = []
-        for n, (pair, c0, w) in enumerate(HUB_LOADS):
-            t = sb.tile([P, 2, w], F32, name="hub_raw%d" % n, align_bytes=64)
-            nc.sync.dma_start(t[:], hub_rows[:, 2 * pair:2 * pair + 2, c0:c0 + w])
+        for n, (c0, w) in enumerate(PAIR_LOADS):
+            t = sb.tile([P, 2, w], F32, name="pair_raw%d" % n, align_bytes=64)
+            nc.sync.dma_start(t[:], hub_rows[:, 2:4, c0:c0 + w])
             raw.append(t)
-            if n == 0:
-                nc.sync.dma_start(tie_list[:], offs)
-                nc.sync.dma_start(tie_bytes[0:P:8, :].bitcast(I32), ties_scales[0].bitcast(I32))
-                nc.sync.dma_start(hub_list[:], offs2)
 
         q_raw = sb.tile([P, PACK, Q], F32, name="q_raw", align_bytes=64)
         nc.sync.dma_start(q_raw[:], query.rearrange("(p t) q -> p t q", t=PACK))
+        hf_sb = sb.tile([P, PACK], F32, name="hf_sb", tag="hp_then_words", align_bytes=64)
+        nc.sync.dma_start(hf_sb[:], hf.rearrange("(p r) o -> p (r o)", r=PACK))
         tie_words = sb.tile([P, T], I32, name="tie_words", align_bytes=64)
         nc.sync.dma_start(tie_words[:], ties_words[0].rearrange("p n t -> p (n t)").bitcast(I32))
+        hub_bf = sb.tile([P, J * PACK], BF16, name="hub_bf", align_bytes=64)
+        dealt_values = hub_bf[:].rearrange("p (r m t) -> p t m r", r=PACK, t=PACK)
+        plane_bf = [sb.tile([P, U], BF16, name="plane_bf%d" % t, align_bytes=64) for t in range(2)]
+        nc.vector.tensor_copy(out=plane_bf[0][:], in_=plane_raw[0][:])
+        nc.scalar.activation(out=dealt_values[:, 0], in_=plane_bf[0][:].indirect(hub_list[:]), func=ACT.Copy)
         got_bytes = sb.tile([P, I], U8, name="got_bytes", align_bytes=64)
         nc.vector.tensor_copy(out=got_bytes[:], in_=tie_bytes[:].indirect(tie_list[:]))
         for r in range(4):
             nc.sync.dma_start(tie_plane[r:P:32, :].bitcast(I32), got_bytes[8 * r:P:32, :].bitcast(I32))
-        hf_sb = sb.tile([P, PACK], F32, name="hf_sb")
-        nc.sync.dma_start(hf_sb[:], hf.rearrange("(p r) o -> p (r o)", r=PACK))
         nc.sync.dma_start(place_list[:], offs3)
         fade_sb = sb.tile([P, 1], F32, name="fade_sb")
         nc.sync.dma_start(fade_sb[:], fade)
@@ -72,22 +78,14 @@ def tile_attend_relayed_soft_counts_kernel(tc, query, hubs, hf, ties_words, ties
         nc.sync.dma_start(old_sb[:], old)
 
 
-        hub_bf = sb.tile([P, J * PACK], BF16, name="hub_bf", align_bytes=64)
-        dealt = hub_bf[:].bitcast(U32).rearrange("p (r m u) -> p u m r", r=PACK, u=2)
-        pairs = [sb.tile([P, U * 2], BF16, name="pair%d" % u, align_bytes=64) for u in range(2)]
-        for u in range(2):
-            for n, a, w, eng in HUB_CASTS:
-                pair, base, whole = HUB_LOADS[n]
-                if pair != u:
-                    continue
-                c0 = base + a
-                dst = pairs[u][:, 2 * c0:2 * (c0 + w)].rearrange("p (c t) -> p c t", t=2)
-                src = raw[n][:, :, a:a + w].rearrange("p t c -> p c t")
-                if eng == "s":
-                    nc.scalar.activation(out=dst, in_=src, func=ACT.Copy)
-                else:
-                    nc.vector.tensor_copy(out=dst, in_=src)
-            nc.vector.tensor_copy(out=dealt[:, u], in_=pairs[u][:].bitcast(U32).indirect(hub_list[:]))
+        nc.vector.tensor_copy(out=plane_bf[1][:], in_=plane_raw[1][:])
+        nc.scalar.activation(out=dealt_values[:, 1], in_=plane_bf[1][:].indirect(hub_list[:]), func=ACT.Copy)
+        dealt_words = hub_bf[:].bitcast(U32).rearrange("p (r m u) -> p u m r", r=PACK, u=2)
+        pair = sb.tile([P, U * 2], BF16, name="pair", align_bytes=64)
+        for n, (c0, w) in enumerate(PAIR_LOADS):
+            nc.vector.tensor_copy(out=pair[:, 2 * c0:2 * (c0 + w)].rearrange("p (c t) -> p c t", t=2),
+                                  in_=raw[n][:].rearrange("p t c -> p c t"))
+        nc.vector.tensor_copy(out=dealt_words[:, 1], in_=pair[:].bitcast(U32).indirect(hub_list[:]))
 
         q_bf = sb.tile([P, Q, PACK], BF16, name="q_bf", align_bytes=64)
         nc.scalar.activation(out=q_bf[:], in_=q_raw[:].rearrange("p t q -> p q t"), func=ACT.Copy)
@@ -109,7 +107,7 @@ def tile_attend_relayed_soft_counts_kernel(tc, query, hubs, hf, ties_words, ties
         words_lo = sb.tile([P, H], U32, name="words_lo", align_bytes=64)
         nc.vector.tensor_copy(out=words_lo[:], in_=tie_words[:].bitcast(U32).indirect(tie_list[:, 0:H // 16]))
 
-        hp_bf = sb.tile([P, Q, PACK], BF16, name="hp_bf", tag="hp_then_words", align_bytes=64)
+        hp_bf = sb.tile([P, Q, PACK], BF16, name="hp_bf", align_bytes=64)
         nc.vector.scalar_tensor_tensor(out=hp_bf[:], in0=hb[:].rearrange("p r q -> p q r"), scalar=0.0,
                                        in1=hf_sb[:].unsqueeze(1).to_broadcast([P, Q, PACK]), op0=ALU.max, op1=ALU.mult)
         hp_codes = sb.tile([P, Q], U32, name="hp_codes", align_bytes=64)

@@ -38,15 +38,10 @@ def tile_attend_relayed_soft_counts_kernel(tc, query, hubs, hf, ties_words, ties
         placed = sb.tile([P, M], F32, name="placed", align_bytes=64)
         nc.vector.memset(placed[:], 0.0)
 
-        warm_in = sb.tile([P, 1], F32, name="warm_in")
-        warm_out = sb.tile([P, 1], F32, name="warm_out")
-        nc.gpsimd.memset(warm_in[:], 0.0)
-        nc.scalar.activation(out=warm_out[:], in_=warm_in[:], func=ACT.Exp)
-
         hub_rows = hubs.rearrange("(p t) u -> p t u", t=PACK)
         plane_raw = [sb.tile([P, U], F32, name="plane_raw%d" % t, align_bytes=64) for t in range(2)]
-        nc.sync.dma_start(plane_raw[0][:], hub_rows[:, 0, :])
         nc.sync.dma_start(hub_list[:], offs2)
+        nc.sync.dma_start(plane_raw[0][:], hub_rows[:, 0, :])
         nc.sync.dma_start(tie_list[:], offs)
         nc.sync.dma_start(tie_bytes[0:P:8, :].bitcast(I32), ties_scales[0].bitcast(I32))
         nc.sync.dma_start(plane_raw[1][:], hub_rows[:, 1, :])
@@ -58,10 +53,10 @@ def tile_attend_relayed_soft_counts_kernel(tc, query, hubs, hf, ties_words, ties
 
         q_raw = sb.tile([P, PACK, Q], F32, name="q_raw", align_bytes=64)
         nc.sync.dma_start(q_raw[:], query.rearrange("(p t) q -> p t q", t=PACK))
-        hf_sb = sb.tile([P, PACK], F32, name="hf_sb", tag="hp_then_words", align_bytes=64)
-        nc.sync.dma_start(hf_sb[:], hf.rearrange("(p r) o -> p (r o)", r=PACK))
         tie_words = sb.tile([P, T], I32, name="tie_words", align_bytes=64)
         nc.sync.dma_start(tie_words[:], ties_words[0].rearrange("p n t -> p (n t)").bitcast(I32))
+        hf_sb = sb.tile([P, PACK], F32, name="hf_sb", tag="hp_then_words", align_bytes=64)
+        nc.sync.dma_start(hf_sb[:], hf.rearrange("(p r) o -> p (r o)", r=PACK))
         hub_bf = sb.tile([P, J * PACK], BF16, name="hub_bf", align_bytes=64)
         dealt_values = hub_bf[:].rearrange("p (r m t) -> p t m r", r=PACK, t=PACK)
         plane_bf = [sb.tile([P, U], BF16, name="plane_bf%d" % t, align_bytes=64) for t in range(2)]

from contextlib import ExitStack

import concourse.mybir as mybir

D, T, I, Q, J, U, M = 512, 2048, 512, 128, 512, 1024, 2048
FLOPS = 2 * D * J * Q + 2 * J * Q * I

F32 = mybir.dt.float32
BF16 = mybir.dt.bfloat16
I32 = mybir.dt.int32
U32 = mybir.dt.uint32
U16 = mybir.dt.uint16
U8 = mybir.dt.uint8
FP8X4 = mybir.dt.float8_e4m3fn_x4
ALU = mybir.AluOpType
ACT = mybir.ActivationFunctionType
P = 128
PACK = 4

PAIR_LOADS = [(0, 512), (512, 256), (768, 256)]
OUT_CHUNKS = [256, 512, 512, 512, 256]


def tile_attend_relayed_soft_counts_kernel(tc, query, hubs, hf, ties_words, ties_scales, old, fade, offs, offs2, offs3, out):
    nc = tc.nc
    with ExitStack() as ctx:
        sb = ctx.enter_context(tc.tile_pool(name="sb", bufs=1))
        psum = ctx.enter_context(tc.psum_pool(name="psum", bufs=1))

        tie_list = sb.tile([P, I // 16], U16, name="tie_list")
        hub_list = sb.tile([P, J // 16], U16, name="hub_list")
        place_list = sb.tile([P, I // 16], U16, name="place_list")

        tie_bytes = sb.tile([P, T], U8, name="tie_bytes", align_bytes=64)
        nc.vector.memset(tie_bytes[:].bitcast(I32), 0)
        tie_plane = sb.tile([P, I], U8, name="tie_plane", align_bytes=64)
        nc.vector.memset(tie_plane[:].bitcast(I32), 0)
        placed = sb.tile([P, M], F32, name="placed", align_bytes=64)
        nc.vector.memset(placed[:], 0.0)

        hub_rows = hubs.rearrange("(p t) u -> p t u", t=PACK)
        plane_raw = [sb.tile([P, U], F32, name="plane_raw%d" % t, align_bytes=64) for t in range(2)]
        nc.sync.dma_start(hub_list[:], offs2)
        nc.sync.dma_start(plane_raw[0][:], hub_rows[:, 0, :])
        nc.sync.dma_start(tie_list[:], offs)
        nc.sync.dma_start(tie_bytes[0:P:8, :].bitcast(I32), ties_scales[0].bitcast(I32))
        nc.sync.dma_start(plane_raw[1][:], hub_rows[:, 1, :])
        raw = []
        for n, (c0, w) in enumerate(PAIR_LOADS):
            t = sb.tile([P, 2, w], F32, name="pair_raw%d" % n, align_bytes=64)
            nc.sync.dma_start(t[:], hub_rows[:, 2:4, c0:c0 + w])
            raw.append(t)

        q_raw = sb.tile([P, PACK, Q], F32, name="q_raw", align_bytes=64)
        nc.sync.dma_start(q_raw[:], query.rearrange("(p t) q -> p t q", t=PACK))
        tie_words = sb.tile([P, T], I32, name="tie_words", align_bytes=64)
        nc.sync.dma_start(tie_words[:], ties_words[0].rearrange("p n t -> p (n t)").bitcast(I32))
        hf_sb = sb.tile([P, PACK], F32, name="hf_sb", tag="hp_then_words", align_bytes=64)
        nc.sync.dma_start(hf_sb[:], hf.rearrange("(p r) o -> p (r o)", r=PACK))
        hub_bf = sb.tile([P, J * PACK], BF16, name="hub_bf", align_bytes=64)
        dealt_values = hub_bf[:].rearrange("p (r m t) -> p t m r", r=PACK, t=PACK)
        plane_bf = [sb.tile([P, U], BF16, name="plane_bf%d" % t, align_bytes=64) for t in range(2)]
        nc.vector.tensor_copy(out=plane_bf[0][:], in_=plane_raw[0][:])
        nc.scalar.activation(out=dealt_values[:, 0], in_=plane_bf[0][:].indirect(hub_list[:]), func=ACT.Copy)
        got_bytes = sb.tile([P, I], U8, name="got_bytes", align_bytes=64)
        nc.vector.tensor_copy(out=got_bytes[:], in_=tie_bytes[:].indirect(tie_list[:]))
        for r in range(4):
            nc.sync.dma_start(tie_plane[r:P:32, :].bitcast(I32), got_bytes[8 * r:P:32, :].bitcast(I32))
        nc.sync.dma_start(place_list[:], offs3)
        fade_sb = sb.tile([P, 1], F32, name="fade_sb")
        nc.sync.dma_start(fade_sb[:], fade)
        old_sb = sb.tile([P, M], F32, name="old_sb", align_bytes=64)
        nc.sync.dma_start(old_sb[:], old)


        nc.vector.tensor_copy(out=plane_bf[1][:], in_=plane_raw[1][:])
        nc.scalar.activation(out=dealt_values[:, 1], in_=plane_bf[1][:].indirect(hub_list[:]), func=ACT.Copy)
        dealt_words = hub_bf[:].bitcast(U32).rearrange("p (r m u) -> p u m r", r=PACK, u=2)
        pair = sb.tile([P, U * 2], BF16, name="pair", align_bytes=64)
        for n, (c0, w) in enumerate(PAIR_LOADS):
            nc.vector.tensor_copy(out=pair[:, 2 * c0:2 * (c0 + w)].rearrange("p (c t) -> p c t", t=2),
                                  in_=raw[n][:].rearrange("p t c -> p c t"))
        nc.vector.tensor_copy(out=dealt_words[:, 1], in_=pair[:].bitcast(U32).indirect(hub_list[:]))

        q_bf = sb.tile([P, Q, PACK], BF16, name="q_bf", align_bytes=64)
        nc.scalar.activation(out=q_bf[:], in_=q_raw[:].rearrange("p t q -> p q t"), func=ACT.Copy)
        q_codes = sb.tile([P, Q], U32, name="q_codes", align_bytes=64)
        q_scales = sb.tile([P, Q], U8, name="q_scales", align_bytes=64)
        nc.vector.quantize_mx(out=q_codes[:].bitcast(FP8X4), scales=q_scales[:], in_=q_bf[:].rearrange("p q t -> p (q t)"))

        h_codes = sb.tile([P, J], U32, name="h_codes", align_bytes=64)
        h_scales = sb.tile([P, J], U8, name="h_scales", align_bytes=64)
        hb = psum.tile([P, PACK, Q], F32, name="hb")
        for r in range(PACK):
            cols = slice(r * P, (r + 1) * P)
            nc.vector.quantize_mx(out=h_codes[:, cols].bitcast(FP8X4), scales=h_scales[:, cols],
                                  in_=hub_bf[:, r * P * PACK:(r + 1) * P * PACK])
            nc.tensor.matmul_mx(out=hb[:, r, :], lhsT=h_codes[:, cols].bitcast(FP8X4), lhsT_scale=h_scales[:, cols],
                                rhs=q_codes[:].bitcast(FP8X4), rhs_scale=q_scales[:], start=True, stop=True)

        H = I // 2
        words_lo = sb.tile([P, H], U32, name="words_lo", align_bytes=64)
        nc.vector.tensor_copy(out=words_lo[:], in_=tie_words[:].bitcast(U32).indirect(tie_list[:, 0:H // 16]))

        hp_bf = sb.tile([P, Q, PACK], BF16, name="hp_bf", align_bytes=64)
        nc.vector.scalar_tensor_tensor(out=hp_bf[:], in0=hb[:].rearrange("p r q -> p q r"), scalar=0.0,
                                       in1=hf_sb[:].unsqueeze(1).to_broadcast([P, Q, PACK]), op0=ALU.max, op1=ALU.mult)
        hp_codes = sb.tile([P, Q], U32, name="hp_codes", align_bytes=64)
        hp_scales = sb.tile([P, Q], U8, name="hp_scales", align_bytes=64)
        nc.vector.quantize_mx(out=hp_codes[:].bitcast(FP8X4), scales=hp_scales[:], in_=hp_bf[:].rearrange("p q t -> p (q t)"))
        words_hi = sb.tile([P, H], U32, name="words_hi", tag="hp_then_words", align_bytes=64)
        nc.vector.tensor_copy(out=words_hi[:], in_=tie_words[:].bitcast(U32).indirect(tie_list[:, H // 16:I // 16]))

        s = [psum.tile([P, H], F32, name="s%d" % h) for h in range(2)]
        for h, words in enumerate((words_lo, words_hi)):
            nc.tensor.matmul_mx(out=s[h][:], lhsT=hp_codes[:].bitcast(FP8X4), lhsT_scale=hp_scales[:],
                                rhs=words[:].bitcast(FP8X4), rhs_scale=tie_plane[:, h * H:(h + 1) * H], start=True, stop=True)

        neg_lo = sb.tile([P, 1], F32, name="neg_lo")
        nc.vector.tensor_reduce(out=neg_lo[:], in_=s[0][:], axis=mybir.AxisListType.X, op=ALU.max, negate=True)
        neg_max = sb.tile([P, 1], F32, name="neg_max")
        neg_hi = sb.tile([P, H], F32, name="neg_hi", align_bytes=64)
        nc.vector.tensor_scalar(out=neg_hi[:], in0=s[1][:], scalar1=-1.0, scalar2=neg_lo[:], op0=ALU.mult, op1=ALU.min, accum_out=neg_max[:])
        p = sb.tile([P, I], F32, name="p", align_bytes=64)
        for h in range(2):
            nc.scalar.activation(out=p[:, h * H:(h + 1) * H], in_=s[h][:], func=ACT.Exp, bias=neg_max[:])
        p_small = sb.tile([P, I], F32, name="p_small", align_bytes=64)
        total = sb.tile([P, 1], F32, name="total")
        nc.scalar.activation(out=p_small[:], in_=p[:], func=ACT.Copy, scale=1.0 / 256.0, accum_out=total[:])
        nc.vector.tensor_copy(out=placed[:].indirect(place_list[:]), in_=p[:])
        gain = sb.tile([P, 1], F32, name="gain")
        nc.vector.reciprocal(out=gain[:], in_=total[:])

        c0 = 0
        for n, w in enumerate(OUT_CHUNKS):
            cols = slice(c0, c0 + w)
            faded = sb.tile([P, w], F32, name="faded%d" % n, align_bytes=64)
            nc.scalar.activation(out=faded[:], in_=old_sb[:, cols], func=ACT.Copy, scale=fade_sb[:])
            res = sb.tile([P, w], F32, name="res%d" % n, align_bytes=64)
            nc.vector.scalar_tensor_tensor(out=res[:], in0=placed[:, cols], scalar=gain[:], in1=faded[:],
                                           op0=ALU.mult, op1=ALU.add)
            nc.sync.dma_start(out[:, cols], res[:])
            c0 = c0 + w
